import numpy as np
import ml_dtypes


def mxq(x, axis, fmt="e4m3"):
    dtype, down = {"e4m3": (ml_dtypes.float8_e4m3fn, 7), "e5m2": (ml_dtypes.float8_e5m2, 14)}[fmt]
    v = np.moveaxis(np.asarray(x, np.float32).astype(ml_dtypes.bfloat16).astype(np.float64), axis, -1)
    blocks = v.reshape(v.shape[:-1] + (-1, 32))
    amax = np.abs(blocks).max(-1, keepdims=True)
    byte = np.maximum(np.where(amax > 0, np.frexp(amax)[1] - 1 + 127, 0) - down, 1)
    scale = np.exp2(byte - 127.0)
    codes = (blocks / scale).astype(np.float32).astype(dtype).astype(np.float64)
    return np.moveaxis((codes * scale).reshape(v.shape), -1, axis)


WIDE = False


def mx_kscale(k):
    if not WIDE:
        return np.ones(k)
    levels = np.array([10, -10, 5, -5, 0])
    if k % 512:
        return np.exp2(np.random.permutation(np.resize(levels, k // 32))).repeat(32)
    a = np.empty((k // 512, 16))
    for p in range(k // 512):
        a[p, :8] = np.random.permutation(np.resize(levels, 8))
        for g in range(8):
            far = levels[np.abs(levels - a[p, g]) >= 10]
            a[p, g + 8] = far[np.random.randint(len(far))]
    return np.exp2(a.ravel()).repeat(32)


def f64(x):
    return np.asarray(x).astype(np.float64)


def striped(idx):
    return np.tile(idx.reshape(-1, 16).T, (8, 1)).astype(np.uint16)


def unstriped(offs):
    return offs[:16].T.reshape(-1).astype(np.int64)


E2M1 = np.array([0.0, 0.5, 1.0, 1.5, 2.0, 3.0, 4.0, 6.0, -0.0, -0.5, -1.0, -1.5, -2.0, -3.0, -4.0, -6.0])


def pack_weight(w, fmt):
    k, n = w.shape
    w = f64(np.asarray(w, np.float32).astype(ml_dtypes.bfloat16)).reshape(k // 32, 32, n)
    amax = np.abs(w).max(1)
    if fmt == "e4m3":
        byte = np.frexp(amax)[1] - 1 + 127 - 7
    else:
        mant, ex = np.frexp(amax / 6.0)
        byte = np.where(mant > 0.5, ex, ex - 1) + 127
    byte = np.clip(np.where(amax > 0, byte, 1), 1, 254)
    scaled = (w * np.exp2(127.0 - byte)[:, None, :]).reshape(k, n).astype(np.float32)
    by_word = np.ascontiguousarray(scaled.reshape(k // 512, 128, 4, n).transpose(0, 1, 3, 2))
    if fmt == "e4m3":
        words = by_word.astype(ml_dtypes.float8_e4m3fn).view(np.uint8)
    else:
        c = by_word.astype(ml_dtypes.float4_e2m1fn).view(np.uint8) & 0xF
        words = (c[..., 0::2] | (c[..., 1::2] << 4)).reshape(k // 512, 128, 2 * n)
    return np.ascontiguousarray(words), np.ascontiguousarray(byte.astype(np.uint8).reshape(k // 512, 16, n))


def unpack_weight(words, scales, fmt):
    g, _, n = scales.shape
    words = np.ascontiguousarray(words).reshape(g, 128, n, -1)
    if fmt == "e4m3":
        vals = words.view(ml_dtypes.float8_e4m3fn).astype(np.float64)
    else:
        nib = np.empty((g, 128, n, 4), np.uint8)
        nib[..., 0::2] = words & 0xF
        nib[..., 1::2] = words >> 4
        vals = E2M1[nib]
    vals = vals * np.repeat(np.exp2(scales.astype(np.float64) - 127.0), 8, axis=1)[..., None]
    return vals.transpose(0, 1, 3, 2).reshape(g * 512, n)


def gelu(v):
    return 0.5 * v * (1.0 + np.tanh(np.sqrt(2.0 / np.pi) * (v + 0.044715 * v**3)))


K, T, E, C, N = 1024, 1280, 6, 256, 128
TOP = 4
PAD = 64
K8 = 512


def by_expert(wq, xq):
    return np.concatenate([wq[e].T @ xq[:, e * C:(e + 1) * C] for e in range(E)], axis=1)


def setup_inputs():
    n = np.random.standard_normal
    s = mx_kscale(K)[:, None]
    slot_token = np.empty(E * C, np.int64); pos = np.tile(E * C + np.arange(T) % PAD, (TOP, 1)); taken = np.zeros(T, np.int64)
    liked = np.random.randn(T)
    for e in np.random.permutation(E):
        free = np.flatnonzero(taken < TOP); pick = np.random.permutation(free[np.argsort(-(liked[free] + np.random.gumbel(size=free.size)))[:C]]); slot_token[e * C:(e + 1) * C] = pick
        pos[taken[pick], pick] = e * C + np.arange(C); taken[pick] += 1
    g = np.random.uniform(0.2, 0.8, (TOP, T))
    w = n((E, K, N)) / np.sqrt(K) / s[None]
    w8 = [pack_weight(m[:K8], "e4m3") for m in w]
    w4 = [pack_weight(m[K8:], "e2m1") for m in w]
    return {
        "xT": (n((K, T)) * s).astype(np.float32),
        "w8_words": np.stack([m[0] for m in w8]),
        "w8_scales": np.stack([m[1] for m in w8]),
        "w4_words": np.stack([m[0] for m in w4]),
        "w4_scales": np.stack([m[1] for m in w4]),
        "b": (0.3 * n((N, E))).astype(np.float32),
        "gate": np.stack([np.tile(r, (N, 1)) for r in g]).astype(np.float32),
        "offs": striped(slot_token),
        "pos1": striped(pos[0]),
        "pos2": striped(pos[1]),
        "pos3": striped(pos[2]),
        "pos4": striped(pos[3]),
    }


def reference(xT, w8_words, w8_scales, w4_words, w4_scales, b, gate, offs, pos1, pos2, pos3, pos4):
    idx = unstriped(offs)
    w = np.stack([np.concatenate([unpack_weight(w8_words[e], w8_scales[e], "e4m3"), unpack_weight(w4_words[e], w4_scales[e], "e2m1")]) for e in range(E)])
    xq = mxq(f64(xT)[:, idx], 0, "e4m3")
    y = by_expert(w, xq)
    y = gelu(y + np.repeat(f64(b), C, axis=1))
    y = np.concatenate([y, np.zeros((N, PAD))], axis=1)
    return sum(f64(gate[r]) * y[:, unstriped(p)] for r, p in enumerate((pos1, pos2, pos3, pos4)))

@@ -1,0 +1,201 @@
+from contextlib import ExitStack
+
+import concourse.mybir as mybir
+from concourse.masks import make_identity
+
+K, T, E, C, N = 1024, 1280, 6, 256, 128
+TOP = 4
+PAD = 64
+SLOTS = E * C
+FLOPS = 2 * K * N * SLOTS
+
+F32 = mybir.dt.float32
+BF16 = mybir.dt.bfloat16
+I32 = mybir.dt.int32
+U32 = mybir.dt.uint32
+U16 = mybir.dt.uint16
+U8 = mybir.dt.uint8
+FP8X4 = mybir.dt.float8_e4m3fn_x4
+FP4X4 = mybir.dt.float4_e2m1fn_x4
+MULT = mybir.AluOpType.mult
+ADD = mybir.AluOpType.add
+GELU = mybir.ActivationFunctionType.Gelu_apprx_tanh
+COPY = mybir.ActivationFunctionType.Copy
+
+P = 128
+PACK = 4
+K_PASS = P * PACK
+STRIPE = 16
+SCALE_ROW = (4, 0)
+
+X_LOADS = [(0, 0, [("v", 256), ("s", 256)]), (0, 512, [("v", 256), ("s", 256)]), (0, 1024, [("v", 128), ("s", 128)]), (1, 0, [("s", 256), ("s", 256)]), (1, 512, [("v", 256), ("s", 256)]), (1, 1024, [("v", 128), ("s", 128)])]
+WORD0_CUTS = [768, 768]
+BYTE_CUTS = [768, 768]
+WORD1_CUTS = [768, 512, 256]
+PE_CHUNKS = [512, 512]
+LAST_CHUNK = 256
+
+
+def cuts(widths):
+    out = []
+    start = 0
+    for w in widths:
+        out.append((start, start + w))
+        start = start + w
+    return out
+
+
+def tile_moe_ecr_lin_gelu_kernel(tc, xT, w8_words, w8_scales, w4_words, w4_scales, b, gate, offs, pos1, pos2, pos3, pos4, out):
+    nc = tc.nc
+    with ExitStack() as ctx:
+        lists = ctx.enter_context(tc.tile_pool(name="lists", bufs=1))
+        sb = ctx.enter_context(tc.tile_pool(name="sb", bufs=1))
+        psum = ctx.enter_context(tc.psum_pool(name="psum", bufs=1))
+
+        words = [sb.tile([P, T], U32, name="words%d" % a, align_bytes=64) for a in range(2)]
+        scale_bytes = sb.tile([P, T], U8, name="scale_bytes", align_bytes=64)
+        w_scales = sb.tile([P, 2, E, N], U8, name="w_scales", align_bytes=64)
+        y = sb.tile([P, SLOTS + PAD], F32, name="y", align_bytes=64)
+        ident = sb.tile([P, P], F32, name="ident", align_bytes=64)
+        nc.gpsimd.memset(scale_bytes[:].bitcast(I32), 0)
+        nc.gpsimd.memset(w_scales[:].rearrange("p f e n -> p (f e n)").bitcast(I32), 0)
+        nc.gpsimd.memset(y[:, SLOTS:], 0.0)
+        make_identity(nc, ident[:])
+
+        offs_sb = lists.tile([P, SLOTS // STRIPE], U16, name="offs_sb")
+        raws = []
+        for i, (a, t0, shares) in enumerate(X_LOADS):
+            width = sum(w for (eng, w) in shares)
+            raw = sb.tile([P, PACK, width], F32, name="raw%d" % i, align_bytes=64)
+            rows = xT[a * K_PASS:(a + 1) * K_PASS, t0:t0 + width]
+            nc.sync.dma_start(out=raw[:], in_=rows.rearrange("(p j) t -> p j t", j=PACK))
+            raws.append(raw)
+            if i == 2:
+                nc.sync.dma_start(offs_sb[:], offs)
+
+        for f, src in enumerate((w8_scales, w4_scales)):
+            rows = src.rearrange("e a (q r) n -> r q (e a) n", r=4)
+            for r in range(4):
+                nc.sync.dma_start(out=w_scales[r:P:32, f, :, :].bitcast(I32), in_=rows[r].bitcast(I32))
+        w8 = sb.tile([P, E, N * 4], U8, name="w8", align_bytes=64)
+        nc.sync.dma_start(out=w8[:].bitcast(I32), in_=w8_words.rearrange("e a p n r -> p (e a) (n r)").bitcast(I32))
+        w4 = sb.tile([P, E, N * 2], U8, name="w4", align_bytes=64)
+        nc.sync.dma_start(out=w4[:].bitcast(I32), in_=w4_words.rearrange("e a p c -> p (e a) c").bitcast(I32))
+        bias = sb.tile([P, E], F32, name="bias")
+        nc.sync.dma_start(out=bias[:], in_=b)
+        pos_sb = []
+        for r, src in enumerate((pos1, pos2, pos3, pos4)):
+            lst = lists.tile([P, T // STRIPE], U16, name="pos%d" % r)
+            nc.sync.dma_start(lst[:], src)
+            pos_sb.append(lst)
+        token_cuts = cuts(PE_CHUNKS + [LAST_CHUNK])
+        gates = []
+        for i, (t0, t1) in enumerate(token_cuts):
+            g = sb.tile([P, TOP, t1 - t0], F32, name="gate%d" % i, align_bytes=64)
+            nc.sync.dma_start(out=g[:], in_=gate[:, :, t0:t1].rearrange("r p t -> p r t"))
+            gates.append(g)
+
+        def cast_load(i):
+            a, t0, shares = X_LOADS[i]
+            todo = []
+            c0 = 0
+            for s, (eng, w) in enumerate(shares):
+                grouped = sb.tile([P, w * PACK], BF16, name="grouped%d_%d" % (i, s), align_bytes=64)
+                dst = grouped[:].rearrange("p (c i j) -> p c j i", i=4, j=PACK)
+                src = raws[i][:, :, c0:c0 + w].rearrange("p j (c i) -> p c j i", i=4)
+                if eng == "v":
+                    nc.vector.tensor_copy(out=dst, in_=src)
+                else:
+                    nc.scalar.activation(dst, src, COPY)
+                todo.append((grouped, t0 + c0, w))
+                c0 = c0 + w
+            for grouped, s0, w in todo:
+                nc.vector.quantize_mx(out=words[a][:, s0:s0 + w].bitcast(FP8X4), scales=scale_bytes[SCALE_ROW[a]:P, s0:s0 + w], in_=grouped[:])
+
+        def gather(window, dtype, widths, name):
+            pieces = []
+            for i, (s0, s1) in enumerate(cuts(widths)):
+                pieces.append((s0, s1, sb.tile([P, s1 - s0], dtype, name="%s%d" % (name, i), align_bytes=64), window))
+            return pieces
+
+        def run_gather(piece):
+            s0, s1, dst, window = piece
+            nc.vector.tensor_copy(dst[:], window[:].indirect(offs_sb[:, s0 // STRIPE:s1 // STRIPE]))
+
+        def find(pieces, s0):
+            return [(dst, s0 - a0) for (a0, a1, dst, window) in pieces if a0 <= s0 < a1][0]
+
+        gw0 = gather(words[0], U32, WORD0_CUTS, "gw0_")
+        gw1 = gather(words[1], U32, WORD1_CUTS, "gw1_")
+        gb = gather(scale_bytes, U8, BYTE_CUTS, "gb_")
+
+        for i in range(len(X_LOADS)):
+            if X_LOADS[i][0] == 0:
+                cast_load(i)
+        for piece in gw0:
+            run_gather(piece)
+        for i in range(len(X_LOADS)):
+            if X_LOADS[i][0] == 1:
+                cast_load(i)
+
+        def expert(e):
+            acc = psum.tile([P, C], F32, name="acc%d" % e, tag="acc", bufs=3)
+            for h in range(C // P):
+                s0 = e * C + h * P
+                cols = slice(h * P, (h + 1) * P)
+                bt, bo = find(gb, s0)
+                t0, o0 = find(gw0, s0)
+                t1, o1 = find(gw1, s0)
+                nc.tensor.matmul_mx(out=acc[:, cols], lhsT=w8[:, e, :].bitcast(FP8X4), lhsT_scale=w_scales[:, 0, e, :],
+                                    rhs=t0[:, o0:o0 + P].bitcast(FP8X4), rhs_scale=bt[SCALE_ROW[0]:P, bo:bo + P], start=True, stop=False)
+                nc.tensor.matmul_mx(out=acc[:, cols], lhsT=w4[:, e, :].bitcast(FP4X4), lhsT_scale=w_scales[:, 1, e, :],
+                                    rhs=t1[:, o1:o1 + P].bitcast(FP8X4), rhs_scale=bt[SCALE_ROW[1]:P, bo:bo + P], start=False, stop=True)
+            nc.scalar.activation(y[:, e * C:(e + 1) * C], acc[:], GELU, bias=bias[:, e:e + 1])
+
+        done_b = 0
+        next_e = 0
+        for piece in gw1:
+            while done_b < len(gb) and gb[done_b][0] < piece[1]:
+                run_gather(gb[done_b])
+                done_b = done_b + 1
+            run_gather(piece)
+            while next_e < E and (next_e + 1) * C <= piece[1]:
+                expert(next_e)
+                next_e = next_e + 1
+
+        def products(i):
+            t0, t1 = token_cuts[i]
+            prods = []
+            for r in range(TOP):
+                prod = sb.tile([P, t1 - t0], F32, name="prod%d_%d" % (i, r), align_bytes=64)
+                nc.vector.tensor_tensor(prod[:], y[:].indirect(pos_sb[r][:, t0 // STRIPE:t1 // STRIPE]), gates[i][:, r, :], MULT)
+                prods.append(prod)
+            return prods
+
+        for i in range(len(PE_CHUNKS)):
+            t0, t1 = token_cuts[i]
+            blocks = (t1 - t0) // P
+            prods = products(i)
+            sums = [psum.tile([P, P], F32, name="sum%d_%d" % (i, k), tag="sum", bufs=4) for k in range(blocks)]
+            for r in range(TOP):
+                for k in range(blocks):
+                    nc.tensor.matmul(sums[k][:], prods[r][:, k * P:(k + 1) * P], ident[:], start=(r == 0), stop=(r == TOP - 1), is_transpose=True)
+            back = psum.tile([P, t1 - t0], F32, name="back%d" % i, tag="back", bufs=1)
+            for k in range(blocks):
+                turned = sb.tile([P, P], F32, name="turned%d_%d" % (i, k), align_bytes=64)
+                nc.scalar.copy(turned[:], sums[k][:])
+                nc.tensor.transpose(back[:, k * P:(k + 1) * P], turned[:], ident[:])
+            res = sb.tile([P, t1 - t0], F32, name="res%d" % i, align_bytes=64)
+            nc.scalar.copy(res[:], back[:])
+            nc.sync.dma_start(out=out[:, t0:t1], in_=res[:])
+
+        i = len(PE_CHUNKS)
+        t0, t1 = token_cuts[i]
+        prods = products(i)
+        s01 = sb.tile([P, LAST_CHUNK], F32, name="s01", align_bytes=64)
+        s012 = sb.tile([P, LAST_CHUNK], F32, name="s012", align_bytes=64)
+        res = sb.tile([P, LAST_CHUNK], F32, name="res_last", align_bytes=64)
+        nc.vector.tensor_tensor(s01[:], prods[0][:], prods[1][:], ADD)
+        nc.vector.tensor_tensor(s012[:], s01[:], prods[2][:], ADD)
+        nc.vector.tensor_tensor(res[:], s012[:], prods[3][:], ADD)
+        nc.sync.dma_start(out=out[:, t0:t1], in_=res[:])

@@ -28,12 +28,12 @@ K_PASS = P * PACK
 STRIPE = 16
 SCALE_ROW = (4, 0)
 
-X_LOADS = [(0, 0, [("v", 256), ("s", 256)]), (0, 512, [("v", 256), ("s", 256)]), (0, 1024, [("v", 128), ("s", 128)]), (1, 0, [("s", 256), ("s", 256)]), (1, 512, [("v", 256), ("s", 256)]), (1, 1024, [("v", 128), ("s", 128)])]
+X_LOADS = [(0, 0, [[("v", 320), ("s", 192)]]), (0, 512, [[("v", 320), ("s", 192)]]), (0, 1024, [[("v", 112), ("s", 144)]]), (1, 0, [[("s", 512)]]), (1, 512, [[("v", 256), ("s", 256)]]), (1, 1024, [[("s", 256)]])]
 WORD0_CUTS = [768, 768]
 BYTE_CUTS = [768, 768]
-WORD1_CUTS = [768, 512, 256]
-PE_CHUNKS = [512, 512]
-LAST_CHUNK = 256
+WORD1_CUTS = [512, 512, 256, 256]
+PE_CHUNKS = [768, 384]
+LAST_CHUNK = 128
 
 
 def cuts(widths):
@@ -65,7 +65,7 @@ def tile_moe_ecr_lin_gelu_kernel(tc, xT, w8_words, w8_scales, w4_words, w4_scale
         offs_sb = lists.tile([P, SLOTS // STRIPE], U16, name="offs_sb")
         raws = []
         for i, (a, t0, shares) in enumerate(X_LOADS):
-            width = sum(w for (eng, w) in shares)
+            width = sum(w for group in shares for (eng, w) in group)
             raw = sb.tile([P, PACK, width], F32, name="raw%d" % i, align_bytes=64)
             rows = xT[a * K_PASS:(a + 1) * K_PASS, t0:t0 + width]
             nc.sync.dma_start(out=raw[:], in_=rows.rearrange("(p j) t -> p j t", j=PACK))
@@ -95,22 +95,43 @@ def tile_moe_ecr_lin_gelu_kernel(tc, xT, w8_words, w8_scales, w4_words, w4_scale
             nc.sync.dma_start(out=g[:], in_=gate[:, :, t0:t1].rearrange("r p t -> p r t"))
             gates.append(g)
 
+        stage = sb.tile([P, 2 * T * PACK], BF16, name="stage", align_bytes=64)
+        stage_at = []
+        at = 0
+        for a, t0, groups in X_LOADS:
+            row = []
+            for shares in groups:
+                if a == 0 and t0 < 1024:
+                    row.append(at)
+                    at = at + sum(w for (eng, w) in shares) * PACK - 32
+                else:
+                    row.append(None)
+            stage_at.append(row)
+
         def cast_load(i):
-            a, t0, shares = X_LOADS[i]
+            a, t0, groups = X_LOADS[i]
             todo = []
             c0 = 0
-            for s, (eng, w) in enumerate(shares):
-                grouped = sb.tile([P, w * PACK], BF16, name="grouped%d_%d" % (i, s), align_bytes=64)
-                dst = grouped[:].rearrange("p (c i j) -> p c j i", i=4, j=PACK)
-                src = raws[i][:, :, c0:c0 + w].rearrange("p j (c i) -> p c j i", i=4)
-                if eng == "v":
-                    nc.vector.tensor_copy(out=dst, in_=src)
+            for s, shares in enumerate(groups):
+                width = sum(w for (eng, w) in shares)
+                if stage_at[i][s] is None:
+                    own = sb.tile([P, width * PACK], BF16, name="grouped%d_%d" % (i, s), align_bytes=64)
+                    grouped = own[:]
                 else:
-                    nc.scalar.activation(dst, src, COPY)
-                todo.append((grouped, t0 + c0, w))
-                c0 = c0 + w
+                    grouped = stage[:, stage_at[i][s]:stage_at[i][s] + width * PACK]
+                g0 = 0
+                for eng, w in shares:
+                    dst = grouped[:, g0 * PACK:(g0 + w) * PACK].rearrange("p (c i j) -> p c j i", i=2, j=PACK)
+                    src = raws[i][:, :, c0 + g0:c0 + g0 + w].rearrange("p j (c i) -> p c j i", i=2)
+                    if eng == "v":
+                        nc.vector.tensor_copy(out=dst, in_=src)
+                    else:
+                        nc.scalar.copy(dst, src)
+                    g0 = g0 + w
+                todo.append((grouped, t0 + c0, width))
+                c0 = c0 + width
             for grouped, s0, w in todo:
-                nc.vector.quantize_mx(out=words[a][:, s0:s0 + w].bitcast(FP8X4), scales=scale_bytes[SCALE_ROW[a]:P, s0:s0 + w], in_=grouped[:])
+                nc.vector.quantize_mx(out=words[a][:, s0:s0 + w].bitcast(FP8X4), scales=scale_bytes[SCALE_ROW[a]:P, s0:s0 + w], in_=grouped)
 
         def gather(window, dtype, widths, name):
             pieces = []
@@ -138,30 +159,37 @@ def tile_moe_ecr_lin_gelu_kernel(tc, xT, w8_words, w8_scales, w4_words, w4_scale
             if X_LOADS[i][0] == 1:
                 cast_load(i)
 
-        def expert(e):
-            acc = psum.tile([P, C], F32, name="acc%d" % e, tag="acc", bufs=3)
-            for h in range(C // P):
-                s0 = e * C + h * P
-                cols = slice(h * P, (h + 1) * P)
-                bt, bo = find(gb, s0)
-                t0, o0 = find(gw0, s0)
-                t1, o1 = find(gw1, s0)
-                nc.tensor.matmul_mx(out=acc[:, cols], lhsT=w8[:, e, :].bitcast(FP8X4), lhsT_scale=w_scales[:, 0, e, :],
-                                    rhs=t0[:, o0:o0 + P].bitcast(FP8X4), rhs_scale=bt[SCALE_ROW[0]:P, bo:bo + P], start=True, stop=False)
-                nc.tensor.matmul_mx(out=acc[:, cols], lhsT=w4[:, e, :].bitcast(FP4X4), lhsT_scale=w_scales[:, 1, e, :],
-                                    rhs=t1[:, o1:o1 + P].bitcast(FP8X4), rhs_scale=bt[SCALE_ROW[1]:P, bo:bo + P], start=False, stop=True)
-            nc.scalar.activation(y[:, e * C:(e + 1) * C], acc[:], GELU, bias=bias[:, e:e + 1])
+        spans = cuts([256, 256, 256, 256, 256, 128, 128])
+        accs = [psum.tile([P, s1 - s0], F32, name="acc%d" % s0, tag="bank", bufs=8) for (s0, s1) in spans]
 
-        done_b = 0
-        next_e = 0
-        for piece in gw1:
-            while done_b < len(gb) and gb[done_b][0] < piece[1]:
-                run_gather(gb[done_b])
-                done_b = done_b + 1
+        def first_pass(u):
+            s0, s1 = spans[u]
+            e = s0 // C
+            bt, bo = find(gb, s0)
+            t0, o0 = find(gw0, s0)
+            nc.tensor.matmul_mx(out=accs[u][:], lhsT=w8[:, e, :].bitcast(FP8X4), lhsT_scale=w_scales[:, 0, e, :],
+                                rhs=t0[:, o0:o0 + s1 - s0].bitcast(FP8X4), rhs_scale=bt[SCALE_ROW[0]:P, bo:bo + s1 - s0], start=True, stop=False)
+
+        def second_pass(u):
+            s0, s1 = spans[u]
+            e = s0 // C
+            for h0 in range(s0, s1, P):
+                bt, bo = find(gb, h0)
+                t1, o1 = find(gw1, h0)
+                nc.tensor.matmul_mx(out=accs[u][:, h0 - s0:h0 - s0 + P], lhsT=w4[:, e, :].bitcast(FP4X4), lhsT_scale=w_scales[:, 1, e, :],
+                                    rhs=t1[:, o1:o1 + P].bitcast(FP8X4), rhs_scale=bt[SCALE_ROW[1]:P, bo:bo + P], start=False, stop=(h0 + P == s1))
+            nc.scalar.activation(y[:, s0:s1], accs[u][:], GELU, bias=bias[:, e:e + 1])
+
+        for piece in gb:
             run_gather(piece)
-            while next_e < E and (next_e + 1) * C <= piece[1]:
-                expert(next_e)
-                next_e = next_e + 1
+            for u in range(len(spans)):
+                if piece[0] < spans[u][1] <= piece[1]:
+                    first_pass(u)
+        for piece in gw1:
+            run_gather(piece)
+            for u in range(len(spans)):
+                if piece[0] < spans[u][1] <= piece[1]:
+                    second_pass(u)
 
         def products(i):
             t0, t1 = token_cuts[i]
@@ -176,26 +204,28 @@ def tile_moe_ecr_lin_gelu_kernel(tc, xT, w8_words, w8_scales, w4_words, w4_scale
             t0, t1 = token_cuts[i]
             blocks = (t1 - t0) // P
             prods = products(i)
-            sums = [psum.tile([P, P], F32, name="sum%d_%d" % (i, k), tag="sum", bufs=4) for k in range(blocks)]
+            sums = [psum.tile([P, P], F32, name="sum%d_%d" % (i, k), tag="bank", bufs=8) for k in range(blocks)]
             for r in range(TOP):
                 for k in range(blocks):
                     nc.tensor.matmul(sums[k][:], prods[r][:, k * P:(k + 1) * P], ident[:], start=(r == 0), stop=(r == TOP - 1), is_transpose=True)
-            back = psum.tile([P, t1 - t0], F32, name="back%d" % i, tag="back", bufs=1)
-            for k in range(blocks):
-                turned = sb.tile([P, P], F32, name="turned%d_%d" % (i, k), align_bytes=64)
-                nc.scalar.copy(turned[:], sums[k][:])
-                nc.tensor.transpose(back[:, k * P:(k + 1) * P], turned[:], ident[:])
             res = sb.tile([P, t1 - t0], F32, name="res%d" % i, align_bytes=64)
-            nc.scalar.copy(res[:], back[:])
-            nc.sync.dma_start(out=out[:, t0:t1], in_=res[:])
+            for k0 in range(0, blocks, 4):
+                k1 = min(k0 + 4, blocks)
+                back = psum.tile([P, (k1 - k0) * P], F32, name="back%d_%d" % (i, k0), tag="bank", bufs=8)
+                for k in range(k0, k1):
+                    turned = sb.tile([P, P], F32, name="turned%d_%d" % (i, k), align_bytes=64)
+                    nc.scalar.copy(turned[:], sums[k][:])
+                    nc.tensor.transpose(back[:, (k - k0) * P:(k - k0 + 1) * P], turned[:], ident[:])
+                nc.scalar.copy(res[:, k0 * P:k1 * P], back[:])
+            nc.scalar.dma_start(out=out[:, t0:t1], in_=res[:])
 
         i = len(PE_CHUNKS)
         t0, t1 = token_cuts[i]
         prods = products(i)
         s01 = sb.tile([P, LAST_CHUNK], F32, name="s01", align_bytes=64)
-        s012 = sb.tile([P, LAST_CHUNK], F32, name="s012", align_bytes=64)
+        s23 = sb.tile([P, LAST_CHUNK], F32, name="s23", align_bytes=64)
         res = sb.tile([P, LAST_CHUNK], F32, name="res_last", align_bytes=64)
         nc.vector.tensor_tensor(s01[:], prods[0][:], prods[1][:], ADD)
-        nc.vector.tensor_tensor(s012[:], s01[:], prods[2][:], ADD)
-        nc.vector.tensor_tensor(res[:], s012[:], prods[3][:], ADD)
+        nc.vector.tensor_tensor(s23[:], prods[2][:], prods[3][:], ADD)
+        nc.vector.tensor_tensor(res[:], s01[:], s23[:], ADD)
         nc.sync.dma_start(out=out[:, t0:t1], in_=res[:])

from contextlib import ExitStack

import concourse.mybir as mybir
from concourse.masks import make_identity

K, T, E, C, N = 1024, 1280, 6, 256, 128
TOP = 4
PAD = 64
SLOTS = E * C
FLOPS = 2 * K * N * SLOTS

F32 = mybir.dt.float32
BF16 = mybir.dt.bfloat16
I32 = mybir.dt.int32
U32 = mybir.dt.uint32
U16 = mybir.dt.uint16
U8 = mybir.dt.uint8
FP8X4 = mybir.dt.float8_e4m3fn_x4
FP4X4 = mybir.dt.float4_e2m1fn_x4
MULT = mybir.AluOpType.mult
ADD = mybir.AluOpType.add
GELU = mybir.ActivationFunctionType.Gelu_apprx_tanh
COPY = mybir.ActivationFunctionType.Copy

P = 128
PACK = 4
K_PASS = P * PACK
STRIPE = 16
SCALE_ROW = (4, 0)

X_LOADS = [(0, 0, [[("v", 320), ("s", 192)]]), (0, 512, [[("v", 320), ("s", 192)]]), (0, 1024, [[("v", 112), ("s", 144)]]), (1, 0, [[("s", 512)]]), (1, 512, [[("v", 256), ("s", 256)]]), (1, 1024, [[("s", 256)]])]
WORD0_CUTS = [768, 768]
BYTE_CUTS = [768, 768]
WORD1_CUTS = [512, 512, 256, 256]
PE_CHUNKS = [768, 384]
LAST_CHUNK = 128


def cuts(widths):
    out = []
    start = 0
    for w in widths:
        out.append((start, start + w))
        start = start + w
    return out


def tile_moe_ecr_lin_gelu_kernel(tc, xT, w8_words, w8_scales, w4_words, w4_scales, b, gate, offs, pos1, pos2, pos3, pos4, out):
    nc = tc.nc
    with ExitStack() as ctx:
        lists = ctx.enter_context(tc.tile_pool(name="lists", bufs=1))
        sb = ctx.enter_context(tc.tile_pool(name="sb", bufs=1))
        psum = ctx.enter_context(tc.psum_pool(name="psum", bufs=1))

        words = [sb.tile([P, T], U32, name="words%d" % a, align_bytes=64) for a in range(2)]
        scale_bytes = sb.tile([P, T], U8, name="scale_bytes", align_bytes=64)
        w_scales = sb.tile([P, 2, E, N], U8, name="w_scales", align_bytes=64)
        y = sb.tile([P, SLOTS + PAD], F32, name="y", align_bytes=64)
        ident = sb.tile([P, P], F32, name="ident", align_bytes=64)
        nc.gpsimd.memset(scale_bytes[:].bitcast(I32), 0)
        nc.gpsimd.memset(w_scales[:].rearrange("p f e n -> p (f e n)").bitcast(I32), 0)
        nc.gpsimd.memset(y[:, SLOTS:], 0.0)
        make_identity(nc, ident[:])

        offs_sb = lists.tile([P, SLOTS // STRIPE], U16, name="offs_sb")
        raws = []
        for i, (a, t0, shares) in enumerate(X_LOADS):
            width = sum(w for group in shares for (eng, w) in group)
            raw = sb.tile([P, PACK, width], F32, name="raw%d" % i, align_bytes=64)
            rows = xT[a * K_PASS:(a + 1) * K_PASS, t0:t0 + width]
            nc.sync.dma_start(out=raw[:], in_=rows.rearrange("(p j) t -> p j t", j=PACK))
            raws.append(raw)
            if i == 2:
                nc.sync.dma_start(offs_sb[:], offs)

        for f, src in enumerate((w8_scales, w4_scales)):
            rows = src.rearrange("e a (q r) n -> r q (e a) n", r=4)
            for r in range(4):
                nc.sync.dma_start(out=w_scales[r:P:32, f, :, :].bitcast(I32), in_=rows[r].bitcast(I32))
        w8 = sb.tile([P, E, N * 4], U8, name="w8", align_bytes=64)
        nc.sync.dma_start(out=w8[:].bitcast(I32), in_=w8_words.rearrange("e a p n r -> p (e a) (n r)").bitcast(I32))
        w4 = sb.tile([P, E, N * 2], U8, name="w4", align_bytes=64)
        nc.sync.dma_start(out=w4[:].bitcast(I32), in_=w4_words.rearrange("e a p c -> p (e a) c").bitcast(I32))
        bias = sb.tile([P, E], F32, name="bias")
        nc.sync.dma_start(out=bias[:], in_=b)
        pos_sb = []
        for r, src in enumerate((pos1, pos2, pos3, pos4)):
            lst = lists.tile([P, T // STRIPE], U16, name="pos%d" % r)
            nc.sync.dma_start(lst[:], src)
            pos_sb.append(lst)
        token_cuts = cuts(PE_CHUNKS + [LAST_CHUNK])
        gates = []
        for i, (t0, t1) in enumerate(token_cuts):
            g = sb.tile([P, TOP, t1 - t0], F32, name="gate%d" % i, align_bytes=64)
            nc.sync.dma_start(out=g[:], in_=gate[:, :, t0:t1].rearrange("r p t -> p r t"))
            gates.append(g)

        stage = sb.tile([P, 2 * T * PACK], BF16, name="stage", align_bytes=64)
        stage_at = []
        at = 0
        for a, t0, groups in X_LOADS:
            row = []
            for shares in groups:
                if a == 0 and t0 < 1024:
                    row.append(at)
                    at = at + sum(w for (eng, w) in shares) * PACK - 32
                else:
                    row.append(None)
            stage_at.append(row)

        def cast_load(i):
            a, t0, groups = X_LOADS[i]
            todo = []
            c0 = 0
            for s, shares in enumerate(groups):
                width = sum(w for (eng, w) in shares)
                if stage_at[i][s] is None:
                    own = sb.tile([P, width * PACK], BF16, name="grouped%d_%d" % (i, s), align_bytes=64)
                    grouped = own[:]
                else:
                    grouped = stage[:, stage_at[i][s]:stage_at[i][s] + width * PACK]
                g0 = 0
                for eng, w in shares:
                    dst = grouped[:, g0 * PACK:(g0 + w) * PACK].rearrange("p (c i j) -> p c j i", i=2, j=PACK)
                    src = raws[i][:, :, c0 + g0:c0 + g0 + w].rearrange("p j (c i) -> p c j i", i=2)
                    if eng == "v":
                        nc.vector.tensor_copy(out=dst, in_=src)
                    else:
                        nc.scalar.copy(dst, src)
                    g0 = g0 + w
                todo.append((grouped, t0 + c0, width))
                c0 = c0 + width
            for grouped, s0, w in todo:
                nc.vector.quantize_mx(out=words[a][:, s0:s0 + w].bitcast(FP8X4), scales=scale_bytes[SCALE_ROW[a]:P, s0:s0 + w], in_=grouped)

        def gather(window, dtype, widths, name):
            pieces = []
            for i, (s0, s1) in enumerate(cuts(widths)):
                pieces.append((s0, s1, sb.tile([P, s1 - s0], dtype, name="%s%d" % (name, i), align_bytes=64), window))
            return pieces

        def run_gather(piece):
            s0, s1, dst, window = piece
            nc.vector.tensor_copy(dst[:], window[:].indirect(offs_sb[:, s0 // STRIPE:s1 // STRIPE]))

        def find(pieces, s0):
            return [(dst, s0 - a0) for (a0, a1, dst, window) in pieces if a0 <= s0 < a1][0]

        gw0 = gather(words[0], U32, WORD0_CUTS, "gw0_")
        gw1 = gather(words[1], U32, WORD1_CUTS, "gw1_")
        gb = gather(scale_bytes, U8, BYTE_CUTS, "gb_")

        for i in range(len(X_LOADS)):
            if X_LOADS[i][0] == 0:
                cast_load(i)
        for piece in gw0:
            run_gather(piece)
        for i in range(len(X_LOADS)):
            if X_LOADS[i][0] == 1:
                cast_load(i)

        spans = cuts([256, 256, 256, 256, 256, 128, 128])
        accs = [psum.tile([P, s1 - s0], F32, name="acc%d" % s0, tag="bank", bufs=8) for (s0, s1) in spans]

        def first_pass(u):
            s0, s1 = spans[u]
            e = s0 // C
            bt, bo = find(gb, s0)
            t0, o0 = find(gw0, s0)
            nc.tensor.matmul_mx(out=accs[u][:], lhsT=w8[:, e, :].bitcast(FP8X4), lhsT_scale=w_scales[:, 0, e, :],
                                rhs=t0[:, o0:o0 + s1 - s0].bitcast(FP8X4), rhs_scale=bt[SCALE_ROW[0]:P, bo:bo + s1 - s0], start=True, stop=False)

        def second_pass(u):
            s0, s1 = spans[u]
            e = s0 // C
            for h0 in range(s0, s1, P):
                bt, bo = find(gb, h0)
                t1, o1 = find(gw1, h0)
                nc.tensor.matmul_mx(out=accs[u][:, h0 - s0:h0 - s0 + P], lhsT=w4[:, e, :].bitcast(FP4X4), lhsT_scale=w_scales[:, 1, e, :],
                                    rhs=t1[:, o1:o1 + P].bitcast(FP8X4), rhs_scale=bt[SCALE_ROW[1]:P, bo:bo + P], start=False, stop=(h0 + P == s1))
            nc.scalar.activation(y[:, s0:s1], accs[u][:], GELU, bias=bias[:, e:e + 1])

        for piece in gb:
            run_gather(piece)
            for u in range(len(spans)):
                if piece[0] < spans[u][1] <= piece[1]:
                    first_pass(u)
        for piece in gw1:
            run_gather(piece)
            for u in range(len(spans)):
                if piece[0] < spans[u][1] <= piece[1]:
                    second_pass(u)

        def products(i):
            t0, t1 = token_cuts[i]
            prods = []
            for r in range(TOP):
                prod = sb.tile([P, t1 - t0], F32, name="prod%d_%d" % (i, r), align_bytes=64)
                nc.vector.tensor_tensor(prod[:], y[:].indirect(pos_sb[r][:, t0 // STRIPE:t1 // STRIPE]), gates[i][:, r, :], MULT)
                prods.append(prod)
            return prods

        for i in range(len(PE_CHUNKS)):
            t0, t1 = token_cuts[i]
            blocks = (t1 - t0) // P
            prods = products(i)
            sums = [psum.tile([P, P], F32, name="sum%d_%d" % (i, k), tag="bank", bufs=8) for k in range(blocks)]
            for r in range(TOP):
                for k in range(blocks):
                    nc.tensor.matmul(sums[k][:], prods[r][:, k * P:(k + 1) * P], ident[:], start=(r == 0), stop=(r == TOP - 1), is_transpose=True)
            res = sb.tile([P, t1 - t0], F32, name="res%d" % i, align_bytes=64)
            for k0 in range(0, blocks, 4):
                k1 = min(k0 + 4, blocks)
                back = psum.tile([P, (k1 - k0) * P], F32, name="back%d_%d" % (i, k0), tag="bank", bufs=8)
                for k in range(k0, k1):
                    turned = sb.tile([P, P], F32, name="turned%d_%d" % (i, k), align_bytes=64)
                    nc.scalar.copy(turned[:], sums[k][:])
                    nc.tensor.transpose(back[:, (k - k0) * P:(k - k0 + 1) * P], turned[:], ident[:])
                nc.scalar.copy(res[:, k0 * P:k1 * P], back[:])
            nc.scalar.dma_start(out=out[:, t0:t1], in_=res[:])

        i = len(PE_CHUNKS)
        t0, t1 = token_cuts[i]
        prods = products(i)
        s01 = sb.tile([P, LAST_CHUNK], F32, name="s01", align_bytes=64)
        s23 = sb.tile([P, LAST_CHUNK], F32, name="s23", align_bytes=64)
        res = sb.tile([P, LAST_CHUNK], F32, name="res_last", align_bytes=64)
        nc.vector.tensor_tensor(s01[:], prods[0][:], prods[1][:], ADD)
        nc.vector.tensor_tensor(s23[:], prods[2][:], prods[3][:], ADD)
        nc.vector.tensor_tensor(res[:], s01[:], s23[:], ADD)
        nc.sync.dma_start(out=out[:, t0:t1], in_=res[:])
